import numpy as np, ml_dtypes
CORES = [10,34,74,98]
N = 4
import mx_ref
BF = ml_dtypes.bfloat16
def gentries(a):
    return np.ascontiguousarray(a.reshape(8, 16, -1).transpose(0, 2, 1)).reshape(8, -1)
def gtable(e):
    e = np.asarray(e); return np.ascontiguousarray(e.reshape(8, -1, 16).transpose(0, 2, 1)).reshape(128, -1).astype(np.int32)
def gcols(t, e):
    v = np.concatenate([t.reshape(8, 16, -1, 4), np.zeros((8, 16, 1, 4), BF)], axis=2)
    return np.ascontiguousarray(np.stack([v[g][:, e[g]] for g in range(8)])).reshape(128, -1)
def tile(rs):
    return np.stack(rs, axis=2).reshape(128, -1).astype(BF)
def pick(q, e):
    c = np.concatenate([q[0].reshape(128, -1, 4), np.zeros((128, 1, 4), np.uint8)], axis=1); s = np.concatenate([q[1], np.ones((16, 1), np.uint8)], axis=1)
    return (np.ascontiguousarray(c[:, e].reshape(128, -1)), np.ascontiguousarray(s[:, e]))
def join(*qs):
    return (np.concatenate([q[0] for q in qs], axis=1), np.concatenate([q[1] for q in qs], axis=1))
def put(q, e, v):
    c, s = q[0].reshape(128, -1, 4).copy(), q[1].copy(); c[:, e] = v[0].reshape(128, -1, 4); s[:, e] = v[1]
    return (c.reshape(128, -1), s)
def pk(c, s):
    return (np.ascontiguousarray(c), mx_ref.live(s))
def emit(q):
    return q[0], q[1]
def packed(v, rng):
    q = [mx_ref.quantize(np.ascontiguousarray(v[r])) for r in range(N)]
    return np.stack([a for a, b in q]), np.stack([mx_ref.plane(b, rng) for a, b in q])
def values_of_codes():
    e, c = np.zeros((128, 128, 4), np.float32), np.zeros((128, 2, 4), np.uint8)
    e[np.arange(128), np.arange(128), 0] = 1
    c[:127, :, 0] = np.arange(256).reshape(2, 128).T[:127]
    return mx_ref.matmul(mx_ref.quantize(e.reshape(128, 512).astype(BF)), (c.reshape(128, 8), np.full((16, 2), 127, np.uint8))).T.reshape(-1).astype(np.float64)
CODE_VALUE, SCALE_VALUE = values_of_codes(), 2.0 ** (np.arange(256) - 127.0)
def decode(q):
    return (CODE_VALUE[q[0]].reshape(16, 8, -1, 4) * SCALE_VALUE[q[1]][:, None, :, None] + 0.0).reshape(128, -1).astype(np.float32)
def f(rng, *shape):
    return mx_ref.flush((rng.standard_normal(shape, dtype=np.float32) * np.exp2(rng.integers(-2, 3, shape[:-1] + (1,)))).astype(BF))
def wide(rng, *shape, cols=0):
    v = rng.standard_normal(shape, dtype=np.float32) * np.exp2(rng.integers(-12, 13, shape)).astype(np.float32)
    if cols: v *= np.repeat(np.exp2(rng.integers(-cols, cols + 1, shape[:-2] + (1, shape[-1] // 4))) * (rng.random(shape[:-2] + (1, shape[-1] // 4)) > 0.0625), 4, axis=-1).astype(np.float32)
    return mx_ref.flush(v.astype(BF))
C = 480
MASK = [1, 2, 3]
ALIKE = 2
def numbers_of(rng):
    return {"x": np.array(f(rng, N, 128, 4 * C)), "u": np.array(f(rng, N, 128, 512)), "v": np.array(f(rng, N, 128, 512))}
def stored(k):
    return {"se": np.stack([gtable(k[r].reshape(8, 2 * C)) for r in range(N)])}
def lists(rng):
    return stored(rng.permuted(np.tile(np.arange(C), (N, 8, 2, 1)), axis=3))
def layers(rng):
    return np.array(f(rng, N, 128, 2048)).reshape(N, 8, 16, 4, 8, 16, 4)
def weights(rng, w):
    c, s = packed(np.ascontiguousarray(w).reshape(N, 128, 2048), rng)
    return {"wc": c, "ws": s}
def setup_inputs(rng):
    return {**numbers_of(rng), **lists(rng), **weights(rng, layers(rng))}
def setup_inputs_ties(rng):
    d = numbers_of(rng)
    o = rng.permutation(N)
    k = rng.integers(-1, 2, (N, 8, 7, C)).astype(np.float32)
    k[o[1]] = 1
    x = d["x"].reshape(N, 8, 16, C, 4)
    x[:, :, :7, :, 0] = k.astype(BF)
    x[:, :, 8:] = 0
    a = np.exp2(rng.integers(-3, 4, (8, 1)).astype(np.float32))
    x[:, :, 8, :, 0] = (-3.0 * a).astype(BF)
    x[:, :, 10, :, 0] = (-0.0625 * a).astype(BF)
    x[:, :, 11, :, 0] = (0.28125 * a).astype(BF)
    c = np.ones(N, np.float32)
    c[o[0]] = 0
    c[o[2]] = -1
    u = d["u"].reshape(N, 128, 128, 4)
    for l in range(7):
        u[:, :, l::16] = 0
        for h in range(0, 128, 16): u[:, h + l, h + l, 0] = c.astype(BF)
    w = layers(rng)
    w[:, :, :, 0, :, :7] = 0
    w[:, :, :, :, :, 8:] = 0
    for g in range(8):
        w[:, g, 11, 0, g, 8, 0] = 112.0
        for b in range(4): w[:, g, 10, b, g, 9, 0] = -(1.125 + 0.25 * b) * 2.0 ** -5
    return {"x": x.reshape(N, 128, 4 * C), "u": u.reshape(N, 128, 512), "v": d["v"], **lists(rng), **weights(rng, w)}
def setup_inputs_near(rng):
    d = numbers_of(rng)
    k = np.where(((np.arange(N) & ALIKE) > 0) ^ (rng.random() < 0.5), 2.0 ** -30, 1.0)
    x = np.zeros((N, 8, 16, C, 4))
    s = rng.integers(-1, 2, (N, 8, 7, C)) * k[:, None, None, None]
    x[:, :, :7, :, 0] = 1.125 * s
    x[:, :, 8:15, :, 0] = -1.25 * s
    x[:, :, 15] = rng.choice([-1.0, 1.0], (N, 8, C, 4)) * (1.0 + 0.125 * rng.integers(0, 8, (N, 8, C, 4)) * (np.arange(4) > 1)) * 2.0 ** -30
    x[:, :, 15, :, 1] = 2.0 ** -30
    x[:, :, 7, :, 0] = 2.0 ** -30
    for r in range(N):
        at = [0, C - 1, int(rng.integers(C)), int(rng.integers(C))]
        for g, j in zip(rng.permutation(8)[:4], at): x[r, g, int(rng.integers(7)), j, 0] = 2.0 ** 30 * rng.choice([-1.0, 1.0])
    u = d["u"].reshape(N, 128, 128, 4)
    w = np.zeros((N, 8, 16, 4, 8, 16, 4), np.float32)
    for g in range(8):
        w[:, g, 15, 1, g, 7, 0] = 32.0
        w[:, g, 15, 1, g, 15, 1] = 32.0
        w[:, g, 15, 2:, g, 15, 2:] = rng.choice([-1.0, 1.0], (N, 2, 2)) * (8.0 + rng.integers(0, 8, (N, 2, 2)))
    for l in range(7):
        u[:, :, l::16] = 0
        for g in range(8):
            h = 16 * g
            u[:, h + l, h + l, 0] = (1.125 * k).astype(np.float32).astype(BF)
            u[:, h + 8 + l, h + l, 0] = k.astype(np.float32).astype(BF)
            w[:, g, 15, 0, g, l, 0] = rng.choice([-1.0, 1.0], N) * 2.0 ** -8
    return {"x": x.astype(np.float32).reshape(N, 128, 4 * C).astype(BF), "u": u.reshape(N, 128, 512), "v": d["v"], **lists(rng), **weights(rng, w.astype(BF))}
def setup_inputs_odd(rng):
    d = numbers_of(rng)
    x = (1.0 + (2 * rng.integers(0, 64, (N, 8, 16, C, 4)) + 1) * 2.0 ** -7) * np.exp2(-rng.integers(0, 7, (N, 8, 16, C, 4)).astype(np.float64)) * rng.choice([-1.0, 1.0], (N, 8, 16, C, 4))
    n = 2 * rng.integers(4, 8, (N, 8, 7, C)) + 1
    c = rng.choice([-1.0, 1.0], (N, 8, 7, C)) * 2.0 ** -8
    x[:, :, 0, :, 0] = 1.96875 * 2.0 ** 8 * rng.choice([-1.0, 1.0], (N, 8, 1))
    x[:, :, 1:8, :, 0] = c * n
    x[:, :, 8:15, :, 0] = -8.0 * c
    x[:, :, 8:15, :, 1] = -c * (n - 8 + rng.choice([-0.5, 0.5], (N, 8, 7, C)))
    u = d["u"].reshape(N, 128, 128, 4)
    for l in range(7):
        u[:, :, l::16] = 0
        for h in range(0, 128, 16):
            u[:, h + 1 + l, h + l, 0] = 1.0
            u[:, h + 8 + l, h + l, :2] = 1.0
    w = layers(rng)
    w[:, :, :, 0, :, :15] = 0
    w[:, :, :, 1, :, 8:15] = 0
    w[:, :, 0, :, :, :, 0] = 0
    return {"x": x.astype(np.float32).reshape(N, 128, 4 * C).astype(BF), "u": u.reshape(N, 128, 512), "v": d["v"], **lists(rng), **weights(rng, w)}
def setup_inputs_ends(rng):
    d = numbers_of(rng)
    o = rng.permutation(N) % 4
    j = np.arange(C)
    s = rng.choice([-1.0, 1.0], (N, 128, C, 4))
    s[o == 0] = -1
    s[o == 1] = (1.0 - j % 2 * 2.0)[:, None]
    x = s * (0.83 + 0.02 * rng.random((N, 128, C, 4))) * 2.0 ** 30
    x[o == 3] = -(1.0 + 0.125 * rng.integers(0, 8, (N, 128, C, 4))[o == 3]) * 2.0 ** -30
    size = np.where(o == 3, 2.0 ** -30, 2.0 ** 30)
    a = rng.permuted(np.tile(np.arange(8) % 2 * 2.0 - 1.0, (N, 7, 1)), axis=2).transpose(0, 2, 1) * size[:, None, None]
    for r in range(N): a[r, rng.permutation(8)[:2]] = 0
    u = d["u"].reshape(N, 128, 8, 16, 4)
    u[:, :, :, :7] = a.astype(np.float32).astype(BF)[:, None, :, :, None]
    v = rng.choice([-1.0, 1.0], (N, 128, 512)) * np.where(o % 2 == 0, 2.0 ** 30, 2.0 ** -30)[:, None, None]
    t = np.stack([j, (j + 2) % C, C - 1 - j, (j + 1) % C])
    k = rng.integers(0, 2, (N, 8, 2)) + 2 * (rng.permutation(8) < 4)[:, None]
    w = np.zeros((N, 128, 4, 128, 4), np.float32)
    i = np.arange(128)
    for b in range(4): w[:, i, b, i, b] = np.where(o == 3, 32.0, -1.0)[:, None]
    return {"x": x.astype(np.float32).reshape(N, 128, 4 * C).astype(BF), "u": u.reshape(N, 128, 512), "v": v.astype(np.float32).astype(BF), **stored(t[k]), **weights(rng, w.astype(BF))}
def setup_inputs_spread(rng):
    d = setup_inputs(rng)
    d["x"] = wide(rng, N, 128, 4 * C, cols=6)
    return d
def check_inputs(d):
    b = []
    for k in ("x", "u", "v"):
        a = np.abs(d[k].astype(np.float32))
        if not (np.isfinite(a).all() and ((a == 0) | (a >= 2.0 ** -30) & (a <= 2.0 ** 30)).all()): b.append("a value of " + k)
    none, least, most = [emit(mx_ref.quantize(np.full((128, 16), k, np.float32).astype(BF)))[1][0, 0] for k in (0.0, 2.0 ** -8, 2.0 ** 8)]
    for r in range(N):
        if not (np.sort(gentries(d["se"][r]).reshape(8, 2, C), axis=2) == np.arange(C)).all(): b.append("se: a list that is no permutation")
        if ((d["wc"][r] == 0x7F) | (d["wc"][r] == 0xFF)).any(): b.append("wc: a code that is no number")
        s = mx_ref.live(d["ws"][r])
        if ((s != none) & ((s < least) | (s > most))).any(): b.append("ws: a scale out of range")
    return b
def reference(x, u, v, se, wc, ws):
    qu = [mx_ref.quantize(u[r]) for r in range(N)]
    lay = [pk(wc[r], ws[r]) for r in range(N)]
    sec = [gentries(se[r]).reshape(8, 2, C) for r in range(N)]
    now = [x[r] for r in range(N)]
    g = np.arange(8)[:, None]
    for m in MASK:
        new, out = [], []
        for r in range(N):
            p = r ^ m
            bit = (mx_ref.matmul(qu[r], mx_ref.quantize(now[r])).reshape(8, 16, C)[:, :7] > 0).astype(np.int64)
            i = np.tile(np.arange(C), (8, 1))
            k = i
            for l in range(6):
                b = bit[g, l, i]
                i, k = sec[r][g, b, i], sec[p][g, 1 - b, k]
            end = bit[g, 6, k]
            turn = np.arange(C) ^ end ^ end[:, np.arange(C) ^ 1]
            new.append(np.stack([sec[p][g, 1 - b, turn[g, sec[r][:, b]]] for b in range(2)], axis=1))
            z = mx_ref.quantize(((gcols(now[r], i).astype(np.float32) + gcols(now[r], k).astype(np.float32)) * np.float32(0.5)).astype(BF))
            out.append(mx_ref.quantize(tile([mx_ref.matmul(pick(lay[r], np.arange(128 * b, 128 * b + 128)), z) * np.float32(0.03125) for b in range(4)])))
        now = [(now[r].astype(np.float32) + gcols(decode(out[r ^ m]).astype(BF), new[r][:, 0]).astype(np.float32)).astype(BF) for r in range(N)]
        sec = new
    y, so = np.zeros((N, 128, C), np.float32), np.zeros((N, 8, 2 * C), np.float32)
    oc, osc = np.zeros((N, 128, 4 * C), np.uint8), np.zeros((N, 16, C), np.uint8)
    for r in range(N):
        q = mx_ref.quantize(now[r])
        y[r] = mx_ref.matmul(mx_ref.quantize(v[r]), q)
        so[r] = sec[r].reshape(8, 2 * C)
        oc[r], osc[r] = emit(q)
    return {"y": y, "so": so, "oc": oc, "osc": osc}

@@ -1,0 +1,480 @@
+from concourse.bass import DstId, RemoteDMATransfer
+from concourse.mybir import dt, AluOpType as OP, ActivationFunctionType as AF
+
+C = 480
+CH = [(0, 256), (256, 480)]
+MASK = [1, 2, 3]
+TW = 1056
+
+SCRATCH = {
+    "UT": ("sbuf", [128, 512], "bfloat16"), "VT": ("sbuf", [128, 512], "bfloat16"),
+    "X0": ("sbuf", [128, 4 * C], "bfloat16"), "X1": ("sbuf", [128, 4 * C], "bfloat16"),
+    "X2": ("sbuf", [128, 4 * C], "bfloat16"), "X3": ("sbuf", [128, 4 * C], "bfloat16"),
+    "XH": ("sbuf", [128, 4 * C], "bfloat16"), "G": ("sbuf", [128, 4 * C], "bfloat16"),
+    "Z": ("sbuf", [128, 4 * C], "bfloat16"), "H": ("sbuf", [128, 4 * C], "bfloat16"),
+    "D": ("sbuf", [128, 4 * C], "bfloat16"),
+    "SE": ("sbuf", [128, 60], "int32"), "SN": ("sbuf", [128, 64], "float32"), "SPF": ("sbuf", [128, 32], "float32"),
+    "DS": ("sbuf", [128, 32], "float32"),
+    "TD": ("sbuf", [128, 224], "float32"), "TB": ("sbuf", [128, 224], "float32"),
+    "FT": ("sbuf", [128, 224], "float32"), "FS": ("sbuf", [128, 224], "float32"), "FL": ("sbuf", [128, 224], "uint16"),
+    "A": ("sbuf", [128, 544], "bfloat16"), "YB": ("sbuf", [128, 544], "bfloat16"), "YK": ("sbuf", [128, 544], "bfloat16"),
+    "GA0": ("sbuf", [128, 544], "bfloat16"), "GA1": ("sbuf", [128, 544], "bfloat16"),
+    "TT": ("sbuf", [128, TW], "bfloat16"), "TS": ("sbuf", [128, TW], "bfloat16"), "T2": ("sbuf", [128, 2 * TW], "bfloat16"),
+    "SM": ("sbuf", [128, 1024], "bfloat16"),
+    "CB": ("sbuf", [128, 2 * C], "bfloat16"), "EB": ("sbuf", [128, 2 * C], "bfloat16"), "EA": ("sbuf", [128, 2 * C], "bfloat16"),
+    "Y2": ("sbuf", [128, C], "bfloat16"), "Y1": ("sbuf", [128, C], "bfloat16"), "Y4": ("sbuf", [128, C], "bfloat16"),
+    "WK": ("sbuf", [128, C], "bfloat16"), "WL": ("sbuf", [128, C], "bfloat16"),
+    "ID": ("sbuf", [128, C], "float32"), "ID1": ("sbuf", [128, C], "float32"), "IDB": ("sbuf", [128, C], "float32"),
+    "LG": ("sbuf", [128, C], "float32"), "LV1": ("sbuf", [128, C], "float32"), "LV2": ("sbuf", [128, C], "float32"),
+    "LV3": ("sbuf", [128, C], "float32"),
+    "EN": ("sbuf", [128, C], "bfloat16"), "XX": ("sbuf", [128, C // 2], "bfloat16"), "DD": ("sbuf", [128, C // 2], "float32"),
+    "XD": ("sbuf", [128, C // 2], "float32"), "RR": ("sbuf", [128, C], "float32"),
+    "SOA": ("sbuf", [128, C], "float32"), "SOB": ("sbuf", [128, C], "float32"), "YO": ("sbuf", [128, C], "float32"),
+    "K4": ("sbuf", [128, 64], "uint16"), "K6": ("sbuf", [128, 64], "uint16"),
+    "IC": ("sbuf", [128, 8], "int32"), "CC": ("sbuf", [128, 48], "float32"), "SI": ("sbuf", [128, 32], "float32"),
+    "SEL": ("sbuf", [128, 22], "uint16"), "UL": ("sbuf", [128, 8], "uint16"),
+    "ONE": ("sbuf", [128, 128], "bfloat16"), "EYE": ("sbuf", [128, 128], "bfloat16"), "ET": ("sbuf", [128, 2048], "bfloat16"),
+    "QU": ("sbuf", [128, 128], "float8_e4m3fn_x4"), "PU": ("sbuf", [128, 128], "uint8"),
+    "QUP": ("sbuf", [128, 128], "float8_e4m3fn_x4"), "PUP": ("sbuf", [128, 128], "uint8"),
+    "QV": ("sbuf", [128, 128], "float8_e4m3fn_x4"), "PV": ("sbuf", [128, 128], "uint8"),
+    "QE": ("sbuf", [128, 512], "float8_e4m3fn_x4"), "PE": ("sbuf", [128, 512], "uint8"),
+    "QW": ("sbuf", [128, 512], "float8_e4m3fn_x4"), "PW": ("sbuf", [128, 512], "uint8"),
+    "QX": ("sbuf", [128, C], "float8_e4m3fn_x4"), "PX": ("sbuf", [128, C], "uint8"),
+    "QO": ("sbuf", [128, C], "float8_e4m3fn_x4"), "PO": ("sbuf", [128, C], "uint8"),
+    "QZ": ("sbuf", [128, C], "float8_e4m3fn_x4"), "PZ": ("sbuf", [128, C], "uint8"),
+    "ps": ("psum", [128, 4096], "float32"),
+}
+for _r in range(4):
+    SCRATCH["SU%d" % _r] = ("sbuf", [128, 64], "uint16")
+for _r in range(3):
+    SCRATCH["QH%d" % _r] = ("sbuf", [128, C], "float8_e4m3fn_x4")
+    SCRATCH["PH%d" % _r] = ("sbuf", [128, C], "uint8")
+    SCRATCH["LC%d" % _r] = ("sbuf", [128, C], "float8_e4m3fn_x4")
+    SCRATCH["LS%d" % _r] = ("sbuf", [128, C], "uint8")
+    SCRATCH["LL%d" % _r] = ("sbuf", [128, 64], "uint16")
+NDMA = 32
+SEMAPHORES = (["qv", "qs", "qt", "qg", "sent"] + ["dm%d" % k for k in range(NDMA)]
+              + ["ar%d_%d" % (r, k) for r in range(3) for k in range(len(CH))] + ["ls%d" % r for r in range(3)])
+
+
+def rank_program(g, core, T, topo):
+    rank = T.rank_of(core)
+    if rank is None:
+        return
+    eng = {"v": g.vector, "s": g.scalar, "t": g.tensor, "g": g, "y": g.sync}
+    qsem = {"v": "qv", "s": "qs", "t": "qt", "g": "qg"}
+    cnt = {"qv": 0, "qs": 0, "qt": 0, "qg": 0, "sent": 0}
+    waited = {q: {} for q in eng}
+    recs = {}
+    ndma = [0]
+    alldma = []
+
+    def v(name, lo, hi, st=1):
+        return T[name][:, lo:hi:st], [(name, lo, hi, st)]
+
+    def ind(w, off):
+        return w[0].indirect(off[0]), w[1] + off[1]
+
+    def b8(w):
+        return w[0].bitcast(dt.uint8), w[1]
+
+    def b32(w):
+        return w[0].bitcast(dt.uint32), w[1]
+
+    def meets(a, b):
+        if a[1] >= b[2] or b[1] >= a[2]:
+            return False
+        return not (a[3] == b[3] and a[3] > 1 and (a[1] - b[1]) % a[3])
+
+    def wait(q, sem, val):
+        if waited[q].get(sem, 0) < val:
+            eng[q].wait_ge(T.sem[sem], val)
+            waited[q][sem] = val
+
+    def waits(q, outs, ins, anyway=False):
+        need = {}
+        for w, views in ((1, outs), (0, ins)):
+            for view in views:
+                for reg in view[1]:
+                    hard = w or reg[0] == "ps"
+                    if reg[0] == "ps":
+                        reg = ("ps", reg[1] // 512 * 512, reg[1] // 512 * 512 + 512, 1)
+                    for (rg, isw, sem, val, q2) in recs.get(reg[0], []):
+                        if not meets(rg, reg) or not (isw or hard):
+                            continue
+                        if q2 == q and not anyway and not isw:
+                            continue
+                        need[sem] = max(need.get(sem, 0), val)
+        for sem in need:
+            wait(q, sem, need[sem])
+
+    def note(outs, ins, sem, val, q2):
+        for w, views in ((1, outs), (0, ins)):
+            for view in views:
+                for reg in view[1]:
+                    if reg[0] == "ps":
+                        reg = ("ps", reg[1] // 512 * 512, reg[1] // 512 * 512 + 512, 1)
+                    l = recs.setdefault(reg[0], [])
+                    if w or reg[0] == "ps":
+                        l[:] = [x for x in l if not (x[0][1] >= reg[1] and x[0][2] <= reg[2] and (reg[3] == 1 or (x[0][3] == reg[3] and (x[0][1] - reg[1]) % reg[3] == 0)))]
+                    l.append((reg, 1 if (w or reg[0] == "ps") else 0, sem, val, q2))
+
+    def do(q, fn, outs, ins):
+        waits(q, outs, ins)
+        sem = qsem[q]
+        cnt[sem] += 1
+        fn(eng[q]).then_inc(T.sem[sem], 1)
+        note(outs, ins, sem, cnt[sem], q)
+
+    def dma(q, out, in_):
+        waits(q, [out], [in_], True)
+        sem = "dm%d" % ndma[0]
+        ndma[0] += 1
+        eng[q].dma_start(out[0], in_[0]).then_inc(T.sem[sem], 16)
+        note([out], [in_], sem, 16, "dma" + sem)
+        alldma.append(sem)
+
+    def ext(ap):
+        return ap, []
+
+    def send(dst, out, in_, rsem):
+        waits("g", [], [in_])
+        rid, pid, _ = topo.addr(dst)
+        m = topo.mask(core, dst)
+        g.remote_dma(out[0], in_[0], T.sem[rsem], T.sem.sent, pid, rid, m)
+        cnt["sent"] += len(topo.engines(core, dst))
+
+    def lands(out, rsem, val):
+        note([out], [], rsem, val, "remote")
+
+    def tt(out, a, b, op):
+        do("v", lambda e: e.tensor_tensor(out[0], a[0], b[0], op), [out], [a, b])
+
+    def tsc(out, a, s1, s2, o0, o1=None):
+        ins = [a] + [x for x in (s1, s2) if isinstance(x, tuple)]
+        p = [x[0] if isinstance(x, tuple) else x for x in (s1, s2)]
+        if o1 is None:
+            do("v", lambda e: e.tensor_scalar(out[0], a[0], p[0], None, o0), [out], ins)
+        else:
+            do("v", lambda e: e.tensor_scalar(out[0], a[0], p[0], p[1], o0, o1), [out], ins)
+
+    def tcp(out, a):
+        do("v", lambda e: e.tensor_copy(out[0], a[0]), [out], [a])
+
+    def act(out, a, func=AF.Copy, scale=1.0, bias=0.0):
+        ins = [a] + [x for x in (scale, bias) if isinstance(x, tuple)]
+        kw = {}
+        if isinstance(scale, tuple) or scale != 1.0:
+            kw["scale"] = scale[0] if isinstance(scale, tuple) else scale
+        if isinstance(bias, tuple) or bias != 0.0:
+            kw["bias"] = bias[0] if isinstance(bias, tuple) else bias
+        do("s", lambda e: e.activation(out[0], a[0], func, **kw), [out], ins)
+
+    def fill(out, c):
+        do("v", lambda e: e.memset(out[0], c), [out], [])
+
+    def quant(q, p, x):
+        do("v", lambda e: e.quantize_mx(q[0], p[0], x[0]), [q, p], [x])
+
+    bank = [0]
+
+    def mm(lq, lp, rq, rp, n):
+        o = v("ps", 512 * bank[0], 512 * bank[0] + n)
+        bank[0] = (bank[0] + 1) % 8
+        do("t", lambda e: e.matmul_mx(o[0], lq[0], lp[0], rq[0], rp[0], True, True), [o], [lq, lp, rq, rp])
+        return o
+
+    def turn(dst, at, src):
+        do("v", lambda e: e.transpose(T[dst][:, at:at + C], T[src][:, 32:32 + C]), [v(dst, at, at + C)], [v(src, 32, 32 + C)])
+        do("v", lambda e: e.transpose(T[dst][:, at + C:at + C + 512], T[src][:, 16:528]), [v(dst, at + C, at + C + 512)], [v(src, 16, 528)])
+
+    def col(k):
+        return v("CC", k, k + 1)
+
+    def iota(out, pattern, base, cm):
+        do("g", lambda e: e.iota(out[0], pattern, base, cm, allow_small_or_imprecise_dtypes=True), [out], [])
+
+    dma("s", v("SE", 0, 60), ext(T.se[:]))
+    for lo, hi in CH:
+        dma("y", v("X0", 4 * lo, 4 * hi), ext(T.x[:, 4 * lo:4 * hi]))
+    dma("s", v("UT", 0, 512), ext(T.u[:]))
+    dma("s", b8(v("QW", 0, 512)), ext(T.wc[:]))
+    dma("s", v("PW", 0, 512), ext(T.ws[:]))
+    dma("y", v("VT", 0, 512), ext(T.v[:]))
+
+    do("g", lambda e: e.iota(T.IC[:, 0:1], [[0, 1]], 0, 1), [v("IC", 0, 1)], [])
+    iota(v("SI", 0, 2), [[256, 2]], 7, 0)
+    iota(v("SI", 2, 12), [[1, 5], [256, 2]], 9, 0)
+    iota(v("SI", 12, 14), [[256, 2]], 9, 0)
+    iota(v("SI", 14, 18), [[1, 2], [256, 2]], 7, 0)
+    iota(v("SI", 18, 22), [[TW + 1, 2], [256, 2]], 14, 0)
+    iota(v("SI", 22, 30), [[16, 8]], 0, 0)
+    iota(v("IDB", 0, C), [[1, C]], -240, 0)
+    iota(v("ID", 0, C), [[1, C]], 0, 0)
+
+    ic = lambda k: v("IC", k, k + 1)
+    for k, sh, an in ((1, 0, 15), (2, 0, 1), (3, 1, 1), (4, 2, 1), (5, 4, 1), (6, 1, 7)):
+        tsc(ic(k), ic(0), sh, an, OP.logical_shift_right, OP.bitwise_and)
+    tcp(v("CC", 0, 7), v("IC", 0, 7))
+    tsc(col(7), col(1), 8.0, None, OP.is_lt)
+    tsc(col(8), col(1), 4.0, None, OP.is_lt)
+    tsc(col(9), col(1), 8.0, None, OP.is_equal)
+    tsc(col(30), col(1), -8.0, None, OP.add)
+    tsc(col(33), col(1), 15.0, None, OP.is_equal)
+    tsc(col(15), col(4), -1.0, 1.0, OP.mult, OP.add)
+    tsc(col(11), col(2), -1.0, 1.0, OP.mult, OP.add)
+    tsc(col(31), col(1), 10.0, col(30), OP.is_ge, OP.mult)
+    tsc(col(32), col(9), 6.0, col(7), OP.mult, OP.add)
+    tsc(col(16), col(9), 2.0, None, OP.mult)
+    tsc(col(10), col(2), col(7), None, OP.mult)
+    tsc(col(34), col(31), col(32), col(33), OP.add, OP.subtract)
+    tsc(col(17), col(15), col(7), col(16), OP.mult, OP.add)
+    tsc(col(12), col(11), col(7), None, OP.mult)
+    tsc(v("UL", 0, 8), v("SI", 22, 30), col(34), None, OP.add)
+
+    fill(v("SN", 0, 64), 0.0)
+    fill(v("SM", 0, 1024), 1.0)
+    fill(v("SM", 0, 1024, 8), 0.0)
+    tcp(v("SN", 0, 30), v("SE", 0, 30))
+    tcp(v("SN", 32, 62), v("SE", 30, 60))
+    tcp(v("SU0", 0, 64), v("SN", 0, 64))
+
+    def send_lists(r):
+        dst = T.cores[rank ^ MASK[r]]
+        send(dst, v("LL%d" % r, 0, 64), v("SU%d" % r, 0, 64), "ls%d" % r)
+        lands(v("LL%d" % r, 0, 64), "ls%d" % r, len(topo.engines(dst, core)))
+
+    send_lists(0)
+    for b, lo, hi in [("A", 0, 32), ("A", 512, 544), ("TT", 992, TW), ("YB", 0, 32), ("YB", 512, 544), ("TS", 992, TW), ("YK", 0, 32),
+                      ("YK", 512, 544), ("GA0", 0, 32), ("GA0", 512, 544), ("GA1", 0, 32), ("GA1", 512, 544), ("T2", 992, TW),
+                      ("T2", TW + 992, 2 * TW), ("ET", 0, 2048)]:
+        iota(v(b, lo, hi), [[0, hi - lo]], 0, 0)
+    iota(v("ONE", 0, 128), [[0, 128]], 1, 0)
+    do("g", lambda e: e.affine_select(T.EYE[:, 0:128], T.ONE[:, 0:128], [[-1, 128]], OP.is_equal, 0.0, 0, 1), [v("EYE", 0, 128)], [v("ONE", 0, 128)])
+
+    def tables():
+        tt(v("DS", 0, 32), v("SN", 32, 64), v("SN", 0, 32), OP.subtract)
+        act(v("TB", 0, 32), v("SN", 0, 32))
+        act(v("TB", 32, 64), v("SN", 0, 32))
+        act(v("TD", 0, 32), v("DS", 0, 32))
+        act(v("TD", 32, 64), v("DS", 0, 32))
+        act(v("TB", 64, 128), v("TB", 0, 64))
+        act(v("TB", 128, 192), v("TB", 0, 64))
+        act(v("TD", 64, 128), v("TD", 0, 64), bias=480.0)
+        act(v("TD", 128, 192), v("TD", 0, 64), bias=480.0)
+
+    tables()
+    quant(v("QU", 0, 128), v("PU", 0, 128), v("UT", 0, 512))
+    tcp(b32(v("QUP", 0, 128)), ind(b32(v("QU", 0, 128)), v("UL", 0, 8)))
+    tcp(v("PUP", 0, 128), ind(v("PU", 0, 128), v("UL", 0, 8)))
+
+    def quant_state(r, k):
+        lo, hi = CH[k]
+        q, p = ("QX", "PX") if r < 3 else ("QO", "PO")
+        quant(v(q, lo, hi), v(p, lo, hi), v("X%d" % r, 4 * lo, 4 * hi))
+
+    def signs(k):
+        lo, hi = CH[k]
+        s = mm(v("QUP", 0, 128), v("PUP", 0, 128), v("QX", lo, hi), v("PX", lo, hi), hi - lo)
+        tsc(v("A", 32 + lo, 32 + hi), s, 0.0, col(17), OP.is_gt, OP.not_equal)
+
+    def half_state(r, k):
+        lo, hi = CH[k]
+        for b in range(4):
+            act(v("XH", C * b + lo, C * b + hi), v("X%d" % r, 4 * lo + b, 4 * hi, 4), scale=0.5)
+
+    for k in range(len(CH)):
+        quant_state(0, k)
+
+    tsc(col(25), col(2), col(5), None, OP.not_equal)
+    tsc(col(26), col(5), -32.0, 512.0, OP.mult, OP.add)
+    tsc(col(14), col(3), -1.0, 1.0, OP.mult, OP.add)
+    tsc(col(27), col(25), col(26), None, OP.mult)
+    signs(0)
+    tsc(col(13), col(3), col(7), col(9), OP.mult, OP.add)
+    tsc(col(14), col(14), col(7), col(9), OP.mult, OP.add)
+    tsc(col(28), col(5), 16.0, col(27), OP.mult, OP.add)
+    signs(1)
+    act(v("CB", 0, C), v("IDB", 0, C), AF.Identity, scale=col(9), bias=col(12))
+    act(v("CB", C, 2 * C), v("IDB", 0, C), AF.Identity, scale=col(9), bias=col(10))
+    act(v("ID1", 0, C), v("ID", 0, C), scale=col(11))
+    turn("TT", 0, "A")
+    tsc(col(29), col(6), 32.0, col(28), OP.mult, OP.add)
+    tsc(v("SEL", 0, 22), v("SI", 0, 22), col(29), None, OP.add)
+
+    def more_constants():
+        tsc(col(18), col(3), -512.0, -240.0, OP.mult, OP.add)
+        tsc(col(22), col(3), 2512.0, -2000.0, OP.mult, OP.add)
+        tsc(col(23), col(4), 3024.0, -2000.0, OP.mult, OP.add)
+        tsc(col(19), col(4), -1024.0, col(18), OP.mult, OP.add)
+        tsc(col(21), col(18), col(8), col(9), OP.mult, OP.add)
+        tsc(col(20), col(19), col(7), col(9), OP.mult, OP.add)
+
+    def late_constants():
+        for b in range(4):
+            tcp(v("ET", 512 * b + b, 512 * b + 512, 4), v("EYE", 0, 128))
+        quant(v("QE", 0, 512), v("PE", 0, 512), v("ET", 0, 2048))
+        quant(v("QV", 0, 128), v("PV", 0, 128), v("VT", 0, 512))
+
+    def tables_partner(r):
+        L = "LL%d" % r
+        tcp(v("SPF", 0, 32), v(L, 0, 32))
+        tcp(v("TB", 192, 224), v(L, 32, 64))
+        tt(v("TD", 192, 224), v("SPF", 0, 32), v("TB", 192, 224), OP.subtract)
+
+    def offsets(a, b):
+        lo, hi = 32 * a, 32 * b
+        tt(v("FT", lo, hi), ind(v("TT", 0, TW), v("SEL", 2 * a, 2 * b)), v("TD", lo, hi), OP.mult)
+        tt(v("FS", lo, hi), v("FT", lo, hi), v("TB", lo, hi), OP.add)
+        tcp(v("FL", lo, hi), v("FS", lo, hi))
+
+    def fl(k):
+        return v("FL", 32 * k, 32 * k + 30)
+
+    def level_s(r, k):
+        s0 = v("LL%d" % r, 0, 30)
+        if k == 1:
+            act(v("LG", 0, C), ind(v("ID", 0, C), s0), scale=col(2))
+        else:
+            act(v("LG", 0, C), ind(v("LV%d" % (k - 1), 0, C), s0), AF.Identity, bias=col(20 + k))
+
+    def level_v(r, k):
+        s1 = v("LL%d" % r, 32, 62)
+        if k == 1:
+            tt(v("LV1", 0, C), ind(v("ID1", 0, C), s1), v("LG", 0, C), OP.add)
+        else:
+            tt(v("LV%d" % k, 0, C), ind(v("LV%d" % (k - 1), 0, C), s1), v("LG", 0, C), OP.max)
+
+    def numbers(src, dst):
+        turn("TT", 0, src)
+        do("v", lambda e: e.tensor_tensor_scan(T.TS[:, 0:992], T.SM[:, 0:992], T.TT[:, 0:992], 0.0, OP.mult, OP.add),
+           [v("TS", 0, 992)], [v("SM", 0, 992), v("TT", 0, 992)])
+        tsc(v(dst, 0, 64), ind(v("TS", 0, TW), v("SEL", 14, 18)), 240.0, None, OP.add)
+
+    def outputs(k):
+        lo, hi = CH[k]
+        o = mm(v("QV", 0, 128), v("PV", 0, 128), v("QO", lo, hi), v("PO", lo, hi), hi - lo)
+        dma("y", ext(T.oc[:, 4 * lo:4 * hi]), b8(v("QO", lo, hi)))
+        act(v("YO", lo, hi), o)
+        for j in range(4):
+            dma("s" if j % 2 else "y", ext(T.osc[4 * j:4 * j + 4, lo:hi]), (T.PO[32 * j:32 * j + 4, lo:hi], v("PO", lo, hi)[1]))
+        dma("s", ext(T.y[:, lo:hi]), v("YO", lo, hi))
+
+    for r in range(3):
+        partner = T.cores[rank ^ MASK[r]]
+        X, XN = "X%d" % r, "X%d" % (r + 1)
+        if r == 0:
+            level_s(0, 1)
+            offsets(0, 6)
+            level_v(0, 1)
+        else:
+            turn("TT", 0, "A")
+            offsets(0, 7)
+        tsc(v("EB", 0, C), ind(v("CB", 0, 2 * C), fl(3)), col(14), None, OP.mult)
+        act(v("EB", C, 2 * C), ind(v("CB", 0, 2 * C), fl(3)), scale=col(13))
+        if r == 0:
+            tables_partner(0)
+            offsets(6, 7)
+            more_constants()
+            level_s(0, 2)
+            level_v(0, 2)
+            level_s(0, 3)
+        else:
+            level_v(r, 3)
+        act(v("EA", 0, C), ind(v("CB", 0, 2 * C), fl(5)), scale=col(14))
+        tcp(v("Y2", 0, C), ind(v("EB", 0, 2 * C), fl(2)))
+        if r == 0:
+            level_v(0, 3)
+        tt(v("Y1", 0, C), ind(v("Y2", 0, C), fl(0)), v("A", 32, 32 + C), OP.mult)
+        act(v("WK", 0, C), ind(v("LV3", 0, C), fl(6)), AF.Identity, scale=col(7), bias=col(20))
+        act(v("EA", C, 2 * C), ind(v("CB", 0, 2 * C), fl(5)), scale=col(13))
+        act(v("Y4", 0, C), ind(v("EA", 0, 2 * C), fl(4)))
+        tt(v("YB", 32, 32 + C), ind(v("Y1", 0, C), fl(1)), v("WK", 0, C), OP.mult)
+        numbers("YB", "K4")
+        tt(v("DD", 0, 240), v("LV1", 1, C, 2), v("LV1", 0, C, 2), OP.subtract)
+        act(v("WL", 0, C), ind(v("LV2", 0, C), v("K4", 0, 30)), AF.Identity, scale=col(8), bias=col(21))
+        tt(v("YK", 32, 32 + C), ind(v("Y4", 0, C), v("K4", 32, 62)), v("WL", 0, C), OP.mult)
+        if r == 0:
+            for k in range(len(CH)):
+                half_state(0, k)
+        numbers("YK", "K6")
+        for lo, hi in CH:
+            for b in range(4):
+                act(v("G", C * b + lo, C * b + hi), ind(v("XH", C * b, C * b + C), v("K6", 32 + lo // 16, 32 + hi // 16)))
+        for lo, hi in CH:
+            for b in range(4):
+                tt(v("Z", 4 * lo + b, 4 * hi, 4), ind(v("XH", C * b, C * b + C), v("K6", lo // 16, hi // 16)), v("G", C * b + lo, C * b + hi), OP.add)
+            quant(v("QZ", lo, hi), v("PZ", lo, hi), v("Z", 4 * lo, 4 * hi))
+        for k, (lo, hi) in enumerate(CH):
+            for b in range(4):
+                s = mm(v("QW", 128 * b, 128 * b + 128), v("PW", 128 * b, 128 * b + 128), v("QZ", lo, hi), v("PZ", lo, hi), hi - lo)
+                h = v("H", 4 * lo + b, 4 * hi, 4)
+                if b % 2 == 0:
+                    act(h, s, scale=0.03125)
+                else:
+                    tsc(h, s, 0.03125, None, OP.mult)
+            quant(v("QH%d" % r, lo, hi), v("PH%d" % r, lo, hi), v("H", 4 * lo, 4 * hi))
+            sem = "ar%d_%d" % (r, k)
+            send(partner, b8(v("LC%d" % r, lo, hi)), b8(v("QH%d" % r, lo, hi)), sem)
+            send(partner, v("LS%d" % r, lo, hi), v("PH%d" % r, lo, hi), sem)
+            n = 2 * len(topo.engines(partner, core))
+            lands(v("LC%d" % r, lo, hi), sem, n)
+            lands(v("LS%d" % r, lo, hi), sem, n)
+        act(v("EN", 0, C), ind(v("A", 32, 32 + C), v("K6", 0, 30)))
+        tt(v("XX", 0, 240), v("EN", 0, C, 2), v("EN", 1, C, 2), OP.not_equal)
+        tt(v("XD", 0, 240), v("XX", 0, 240), v("DD", 0, 240), OP.mult)
+        tt(v("RR", 0, C, 2), v("LV1", 0, C, 2), v("XD", 0, 240), OP.add)
+        tt(v("RR", 1, C, 2), v("LV1", 1, C, 2), v("XD", 0, 240), OP.subtract)
+        own0, own1 = v("SU%d" % r, 0, 30), v("SU%d" % r, 32, 62)
+        act(v("GA0", 32, 32 + C), ind(v("RR", 0, C), own0), bias=-240.0)
+        if r < 2:
+            tsc(v("GA1", 32, 32 + C), ind(v("RR", 0, C), own1), -240.0, None, OP.add)
+        else:
+            act(v("SOA", 0, C), ind(v("RR", 0, C), own0))
+            act(v("SOB", 0, C), ind(v("RR", 0, C), own1))
+        turn("T2", 0, "GA0")
+        if r < 2:
+            turn("T2", TW, "GA1")
+        tsc(v("SN", 0, 64), ind(v("T2", 0, 2 * TW), v("SEL", 18, 22)), 240.0, None, OP.add)
+        new = "SU%d" % (r + 1)
+        tcp(v(new, 0, 64), v("SN", 0, 64))
+        if r < 2:
+            send_lists(r + 1)
+            tables()
+        else:
+            dma("y", ext(T.so[:, 0:C]), (T.SOA[14:128:16, 0:C], v("SOA", 0, C)[1]))
+            dma("y", ext(T.so[:, C:2 * C]), (T.SOB[15:128:16, 0:C], v("SOB", 0, C)[1]))
+        if r == 0:
+            late_constants()
+        for k, (lo, hi) in enumerate(CH):
+            for b in range(4):
+                s = mm(v("QE", 128 * b, 128 * b + 128), v("PE", 128 * b, 128 * b + 128), v("LC%d" % r, lo, hi), v("LS%d" % r, lo, hi), hi - lo)
+                d = v("D", C * b + lo, C * b + hi)
+                if b % 2 == 0:
+                    act(d, s)
+                else:
+                    tcp(d, s)
+        for k, (lo, hi) in enumerate(CH):
+            if r < 2:
+                level_s(r + 1, k + 1)
+            for b in range(4):
+                tt(v(XN, 4 * lo + b, 4 * hi, 4), ind(v("D", C * b, C * b + C), v(new, lo // 16, hi // 16)), v(X, 4 * lo + b, 4 * hi, 4), OP.add)
+            quant_state(r + 1, k)
+            if r < 2:
+                half_state(r + 1, k)
+                if k == 0:
+                    level_v(r + 1, 1)
+                else:
+                    signs(0)
+                    level_v(r + 1, 2)
+                    level_s(r + 1, 3)
+                    tables_partner(r + 1)
+                    signs(1)
+            else:
+                outputs(k)
+
+    for sem in alldma:
+        wait("g", sem, 16)
+    for sem in cnt:
+        if cnt[sem]:
+            wait("g", sem, cnt[sem])

@@ -3,6 +3,7 @@ from concourse.mybir import dt, AluOpType as OP, ActivationFunctionType as AF
 
 C = 480
 CH = [(0, 256), (256, 480)]
+GCH = [(0, 320), (320, 480)]
 MASK = [1, 2, 3]
 TW = 1056
 
@@ -19,8 +20,8 @@ SCRATCH = {
     "FT": ("sbuf", [128, 224], "float32"), "FS": ("sbuf", [128, 224], "float32"), "FL": ("sbuf", [128, 224], "uint16"),
     "A": ("sbuf", [128, 544], "bfloat16"), "YB": ("sbuf", [128, 544], "bfloat16"), "YK": ("sbuf", [128, 544], "bfloat16"),
     "GA0": ("sbuf", [128, 544], "bfloat16"), "GA1": ("sbuf", [128, 544], "bfloat16"),
-    "TT": ("sbuf", [128, TW], "bfloat16"), "TS": ("sbuf", [128, TW], "bfloat16"), "T2": ("sbuf", [128, 2 * TW], "bfloat16"),
-    "SM": ("sbuf", [128, 1024], "bfloat16"),
+    "TT": ("sbuf", [128, 2 * TW], "bfloat16"), "T2": ("sbuf", [128, 2 * TW], "bfloat16"),
+    "SM": ("sbuf", [128, 496], "bfloat16"),
     "CB": ("sbuf", [128, 2 * C], "bfloat16"), "EB": ("sbuf", [128, 2 * C], "bfloat16"), "EA": ("sbuf", [128, 2 * C], "bfloat16"),
     "Y2": ("sbuf", [128, C], "bfloat16"), "Y1": ("sbuf", [128, C], "bfloat16"), "Y4": ("sbuf", [128, C], "bfloat16"),
     "WK": ("sbuf", [128, C], "bfloat16"), "WL": ("sbuf", [128, C], "bfloat16"),
@@ -195,7 +196,7 @@ def rank_program(g, core, T, topo):
         do("g", lambda e: e.iota(out[0], pattern, base, cm, allow_small_or_imprecise_dtypes=True), [out], [])
 
     dma("s", v("SE", 0, 60), ext(T.se[:]))
-    for lo, hi in CH:
+    for lo, hi in GCH:
         dma("y", v("X0", 4 * lo, 4 * hi), ext(T.x[:, 4 * lo:4 * hi]))
     dma("s", v("UT", 0, 512), ext(T.u[:]))
     dma("s", b8(v("QW", 0, 512)), ext(T.wc[:]))
@@ -203,38 +204,35 @@ def rank_program(g, core, T, topo):
     dma("y", v("VT", 0, 512), ext(T.v[:]))
 
     do("g", lambda e: e.iota(T.IC[:, 0:1], [[0, 1]], 0, 1), [v("IC", 0, 1)], [])
-    iota(v("SI", 0, 2), [[256, 2]], 7, 0)
-    iota(v("SI", 2, 12), [[1, 5], [256, 2]], 9, 0)
-    iota(v("SI", 12, 14), [[256, 2]], 9, 0)
-    iota(v("SI", 14, 18), [[1, 2], [256, 2]], 7, 0)
-    iota(v("SI", 18, 22), [[TW + 1, 2], [256, 2]], 14, 0)
+    for at, n, row, step in ((0, 2, 7, 4), (4, 2, 5, 4), (8, 2, 14, -11), (12, 1, 3, 0), (14, 2, TW + 14, -TW - 13), (18, 2, 13, TW + 2)):
+        iota(v("SI", at, at + 2 * n), [[step, n], [256, 2]], row, 0)
     iota(v("SI", 22, 30), [[16, 8]], 0, 0)
     iota(v("IDB", 0, C), [[1, C]], -240, 0)
     iota(v("ID", 0, C), [[1, C]], 0, 0)
 
     ic = lambda k: v("IC", k, k + 1)
-    for k, sh, an in ((1, 0, 15), (2, 0, 1), (3, 1, 1), (4, 2, 1), (5, 4, 1), (6, 1, 7)):
+    for k, sh, an in ((1, 0, 15), (2, 1, 1), (3, 2, 1), (4, 3, 1), (5, 4, 1), (6, 1, 7), (7, 0, 1)):
         tsc(ic(k), ic(0), sh, an, OP.logical_shift_right, OP.bitwise_and)
     tcp(v("CC", 0, 7), v("IC", 0, 7))
-    tsc(col(7), col(1), 8.0, None, OP.is_lt)
-    tsc(col(8), col(1), 4.0, None, OP.is_lt)
-    tsc(col(9), col(1), 8.0, None, OP.is_equal)
-    tsc(col(30), col(1), -8.0, None, OP.add)
+    tcp(col(35), ic(7))
+    tsc(col(7), ic(7), -1.0, 1.0, OP.mult, OP.add)
+    tsc(col(9), col(1), 1.0, None, OP.is_equal)
+    tsc(col(30), col(1), 3.0, None, OP.is_equal)
     tsc(col(33), col(1), 15.0, None, OP.is_equal)
     tsc(col(15), col(4), -1.0, 1.0, OP.mult, OP.add)
     tsc(col(11), col(2), -1.0, 1.0, OP.mult, OP.add)
-    tsc(col(31), col(1), 10.0, col(30), OP.is_ge, OP.mult)
-    tsc(col(32), col(9), 6.0, col(7), OP.mult, OP.add)
+    tsc(col(31), col(6), col(30), col(33), OP.subtract, OP.subtract)
     tsc(col(16), col(9), 2.0, None, OP.mult)
     tsc(col(10), col(2), col(7), None, OP.mult)
-    tsc(col(34), col(31), col(32), col(33), OP.add, OP.subtract)
+    tsc(col(8), col(15), col(7), None, OP.mult)
+    tsc(col(34), col(31), col(35), col(7), OP.mult, OP.add)
     tsc(col(17), col(15), col(7), col(16), OP.mult, OP.add)
     tsc(col(12), col(11), col(7), None, OP.mult)
     tsc(v("UL", 0, 8), v("SI", 22, 30), col(34), None, OP.add)
 
     fill(v("SN", 0, 64), 0.0)
-    fill(v("SM", 0, 1024), 1.0)
-    fill(v("SM", 0, 1024, 8), 0.0)
+    fill(v("SM", 0, 496), 1.0)
+    fill(v("SM", 0, 496, 8), 0.0)
     tcp(v("SN", 0, 30), v("SE", 0, 30))
     tcp(v("SN", 32, 62), v("SE", 30, 60))
     tcp(v("SU0", 0, 64), v("SN", 0, 64))
@@ -245,7 +243,7 @@ def rank_program(g, core, T, topo):
         lands(v("LL%d" % r, 0, 64), "ls%d" % r, len(topo.engines(dst, core)))
 
     send_lists(0)
-    for b, lo, hi in [("A", 0, 32), ("A", 512, 544), ("TT", 992, TW), ("YB", 0, 32), ("YB", 512, 544), ("TS", 992, TW), ("YK", 0, 32),
+    for b, lo, hi in [("A", 0, 32), ("A", 512, 544), ("TT", 992, TW), ("YB", 0, 32), ("YB", 512, 544), ("TT", TW, 2 * TW), ("YK", 0, 32),
                       ("YK", 512, 544), ("GA0", 0, 32), ("GA0", 512, 544), ("GA1", 0, 32), ("GA1", 512, 544), ("T2", 992, TW),
                       ("T2", TW + 992, 2 * TW), ("ET", 0, 2048)]:
         iota(v(b, lo, hi), [[0, hi - lo]], 0, 0)
@@ -256,12 +254,12 @@ def rank_program(g, core, T, topo):
         tt(v("DS", 0, 32), v("SN", 32, 64), v("SN", 0, 32), OP.subtract)
         act(v("TB", 0, 32), v("SN", 0, 32))
         act(v("TB", 32, 64), v("SN", 0, 32))
-        act(v("TD", 0, 32), v("DS", 0, 32))
-        act(v("TD", 32, 64), v("DS", 0, 32))
+        act(v("TD", 128, 160), v("DS", 0, 32))
+        act(v("TD", 160, 192), v("DS", 0, 32))
         act(v("TB", 64, 128), v("TB", 0, 64))
         act(v("TB", 128, 192), v("TB", 0, 64))
-        act(v("TD", 64, 128), v("TD", 0, 64), bias=480.0)
-        act(v("TD", 128, 192), v("TD", 0, 64), bias=480.0)
+        act(v("TD", 0, 64), v("TD", 128, 192), bias=480.0)
+        act(v("TD", 64, 128), v("TD", 128, 192), bias=480.0)
 
     tables()
     quant(v("QU", 0, 128), v("PU", 0, 128), v("UT", 0, 512))
@@ -269,24 +267,24 @@ def rank_program(g, core, T, topo):
     tcp(v("PUP", 0, 128), ind(v("PU", 0, 128), v("UL", 0, 8)))
 
     def quant_state(r, k):
-        lo, hi = CH[k]
+        lo, hi = GCH[k]
         q, p = ("QX", "PX") if r < 3 else ("QO", "PO")
         quant(v(q, lo, hi), v(p, lo, hi), v("X%d" % r, 4 * lo, 4 * hi))
 
     def signs(k):
-        lo, hi = CH[k]
+        lo, hi = GCH[k]
         s = mm(v("QUP", 0, 128), v("PUP", 0, 128), v("QX", lo, hi), v("PX", lo, hi), hi - lo)
         tsc(v("A", 32 + lo, 32 + hi), s, 0.0, col(17), OP.is_gt, OP.not_equal)
 
     def half_state(r, k):
-        lo, hi = CH[k]
+        lo, hi = GCH[k]
         for b in range(4):
             act(v("XH", C * b + lo, C * b + hi), v("X%d" % r, 4 * lo + b, 4 * hi, 4), scale=0.5)
 
-    for k in range(len(CH)):
+    for k in range(len(GCH)):
         quant_state(0, k)
 
-    tsc(col(25), col(2), col(5), None, OP.not_equal)
+    tsc(col(25), col(35), col(5), None, OP.not_equal)
     tsc(col(26), col(5), -32.0, 512.0, OP.mult, OP.add)
     tsc(col(14), col(3), -1.0, 1.0, OP.mult, OP.add)
     tsc(col(27), col(25), col(26), None, OP.mult)
@@ -309,12 +307,6 @@ def rank_program(g, core, T, topo):
         tsc(col(19), col(4), -1024.0, col(18), OP.mult, OP.add)
         tsc(col(21), col(18), col(8), col(9), OP.mult, OP.add)
         tsc(col(20), col(19), col(7), col(9), OP.mult, OP.add)
-
-    def late_constants():
-        for b in range(4):
-            tcp(v("ET", 512 * b + b, 512 * b + 512, 4), v("EYE", 0, 128))
-        quant(v("QE", 0, 512), v("PE", 0, 512), v("ET", 0, 2048))
-        quant(v("QV", 0, 128), v("PV", 0, 128), v("VT", 0, 512))
 
     def tables_partner(r):
         L = "LL%d" % r
@@ -347,12 +339,12 @@ def rank_program(g, core, T, topo):
 
     def numbers(src, dst):
         turn("TT", 0, src)
-        do("v", lambda e: e.tensor_tensor_scan(T.TS[:, 0:992], T.SM[:, 0:992], T.TT[:, 0:992], 0.0, OP.mult, OP.add),
-           [v("TS", 0, 992)], [v("SM", 0, 992), v("TT", 0, 992)])
-        tsc(v(dst, 0, 64), ind(v("TS", 0, TW), v("SEL", 14, 18)), 240.0, None, OP.add)
+        o, d, m = v("TT", TW, TW + 992, 2), v("TT", 0, 992, 2), v("SM", 0, 496)
+        do("v", lambda e: e.tensor_tensor_scan(o[0], m[0], d[0], 0.0, OP.mult, OP.add), [o], [m, d])
+        tsc(v(dst, 0, 64), ind(v("TT", 0, 2 * TW), v("SEL", 14, 18)), 240.0, None, OP.add)
 
     def outputs(k):
-        lo, hi = CH[k]
+        lo, hi = GCH[k]
         o = mm(v("QV", 0, 128), v("PV", 0, 128), v("QO", lo, hi), v("PO", lo, hi), hi - lo)
         dma("y", ext(T.oc[:, 4 * lo:4 * hi]), b8(v("QO", lo, hi)))
         act(v("YO", lo, hi), o)
@@ -365,14 +357,14 @@ def rank_program(g, core, T, topo):
         X, XN = "X%d" % r, "X%d" % (r + 1)
         if r == 0:
             level_s(0, 1)
-            offsets(0, 6)
-            level_v(0, 1)
         else:
             turn("TT", 0, "A")
-            offsets(0, 7)
-        tsc(v("EB", 0, C), ind(v("CB", 0, 2 * C), fl(3)), col(14), None, OP.mult)
-        act(v("EB", C, 2 * C), ind(v("CB", 0, 2 * C), fl(3)), scale=col(13))
+        offsets(0, 2)
+        act(v("EB", 0, C), ind(v("CB", 0, 2 * C), fl(0)), scale=col(14))
+        act(v("EB", C, 2 * C), ind(v("CB", 0, 2 * C), fl(0)), scale=col(13))
         if r == 0:
+            offsets(2, 6)
+            level_v(0, 1)
             tables_partner(0)
             offsets(6, 7)
             more_constants()
@@ -380,24 +372,34 @@ def rank_program(g, core, T, topo):
             level_v(0, 2)
             level_s(0, 3)
         else:
+            offsets(2, 7)
             level_v(r, 3)
-        act(v("EA", 0, C), ind(v("CB", 0, 2 * C), fl(5)), scale=col(14))
+        act(v("EA", 0, C), ind(v("CB", 0, 2 * C), fl(1)), scale=col(14))
         tcp(v("Y2", 0, C), ind(v("EB", 0, 2 * C), fl(2)))
         if r == 0:
             level_v(0, 3)
-        tt(v("Y1", 0, C), ind(v("Y2", 0, C), fl(0)), v("A", 32, 32 + C), OP.mult)
+        tt(v("Y1", 0, C), ind(v("Y2", 0, C), fl(4)), v("A", 32, 32 + C), OP.mult)
         act(v("WK", 0, C), ind(v("LV3", 0, C), fl(6)), AF.Identity, scale=col(7), bias=col(20))
-        act(v("EA", C, 2 * C), ind(v("CB", 0, 2 * C), fl(5)), scale=col(13))
-        act(v("Y4", 0, C), ind(v("EA", 0, 2 * C), fl(4)))
-        tt(v("YB", 32, 32 + C), ind(v("Y1", 0, C), fl(1)), v("WK", 0, C), OP.mult)
-        numbers("YB", "K4")
-        tt(v("DD", 0, 240), v("LV1", 1, C, 2), v("LV1", 0, C, 2), OP.subtract)
-        act(v("WL", 0, C), ind(v("LV2", 0, C), v("K4", 0, 30)), AF.Identity, scale=col(8), bias=col(21))
-        tt(v("YK", 32, 32 + C), ind(v("Y4", 0, C), v("K4", 32, 62)), v("WL", 0, C), OP.mult)
+        act(v("EA", C, 2 * C), ind(v("CB", 0, 2 * C), fl(1)), scale=col(13))
+        act(v("Y4", 0, C), ind(v("EA", 0, 2 * C), fl(3)))
+        tt(v("YB", 32, 32 + C), ind(v("Y1", 0, C), fl(5)), v("WK", 0, C), OP.mult)
         if r == 0:
-            for k in range(len(CH)):
+            for b in range(4):
+                act(v("ET", 512 * b + b, 512 * b + 512, 4), v("EYE", 0, 128))
+        if r == 2:
+            quant(v("QV", 0, 128), v("PV", 0, 128), v("VT", 0, 512))
+        numbers("YB", "K4")
+        for lo, hi in CH:
+            act(v("WL", lo, hi), ind(v("LV2", 0, C), v("K4", lo // 16, hi // 16)), AF.Identity, scale=col(8), bias=col(21))
+        tt(v("DD", 0, 240), v("LV1", 1, C, 2), v("LV1", 0, C, 2), OP.subtract)
+        for lo, hi in CH:
+            tt(v("YK", 32 + lo, 32 + hi), ind(v("Y4", 0, C), v("K4", 32 + lo // 16, 32 + hi // 16)), v("WL", lo, hi), OP.mult)
+        if r == 0:
+            for k in range(len(GCH)):
                 half_state(0, k)
         numbers("YK", "K6")
+        if r == 0:
+            quant(v("QE", 0, 512), v("PE", 0, 512), v("ET", 0, 2048))
         for lo, hi in CH:
             for b in range(4):
                 act(v("G", C * b + lo, C * b + hi), ind(v("XH", C * b, C * b + C), v("K6", 32 + lo // 16, 32 + hi // 16)))
@@ -409,7 +411,7 @@ def rank_program(g, core, T, topo):
             for b in range(4):
                 s = mm(v("QW", 128 * b, 128 * b + 128), v("PW", 128 * b, 128 * b + 128), v("QZ", lo, hi), v("PZ", lo, hi), hi - lo)
                 h = v("H", 4 * lo + b, 4 * hi, 4)
-                if b % 2 == 0:
+                if k == 0 or b == 0:
                     act(h, s, scale=0.03125)
                 else:
                     tsc(h, s, 0.03125, None, OP.mult)
@@ -429,9 +431,6 @@ def rank_program(g, core, T, topo):
         act(v("GA0", 32, 32 + C), ind(v("RR", 0, C), own0), bias=-240.0)
         if r < 2:
             tsc(v("GA1", 32, 32 + C), ind(v("RR", 0, C), own1), -240.0, None, OP.add)
-        else:
-            act(v("SOA", 0, C), ind(v("RR", 0, C), own0))
-            act(v("SOB", 0, C), ind(v("RR", 0, C), own1))
         turn("T2", 0, "GA0")
         if r < 2:
             turn("T2", TW, "GA1")
@@ -440,23 +439,21 @@ def rank_program(g, core, T, topo):
         tcp(v(new, 0, 64), v("SN", 0, 64))
         if r < 2:
             send_lists(r + 1)
-            tables()
-        else:
-            dma("y", ext(T.so[:, 0:C]), (T.SOA[14:128:16, 0:C], v("SOA", 0, C)[1]))
-            dma("y", ext(T.so[:, C:2 * C]), (T.SOB[15:128:16, 0:C], v("SOB", 0, C)[1]))
-        if r == 0:
-            late_constants()
         for k, (lo, hi) in enumerate(CH):
             for b in range(4):
                 s = mm(v("QE", 128 * b, 128 * b + 128), v("PE", 128 * b, 128 * b + 128), v("LC%d" % r, lo, hi), v("LS%d" % r, lo, hi), hi - lo)
-                d = v("D", C * b + lo, C * b + hi)
-                if b % 2 == 0:
-                    act(d, s)
-                else:
-                    tcp(d, s)
-        for k, (lo, hi) in enumerate(CH):
-            if r < 2:
-                level_s(r + 1, k + 1)
+                act(v("D", C * b + lo, C * b + hi), s)
+        if r < 2:
+            level_s(r + 1, 1)
+            tables()
+        else:
+            act(v("SOA", 0, C), ind(v("RR", 0, C), own0))
+            act(v("SOB", 0, C), ind(v("RR", 0, C), own1))
+            dma("y", ext(T.so[:, 0:C]), (T.SOA[13:128:16, 0:C], v("SOA", 0, C)[1]))
+            dma("y", ext(T.so[:, C:2 * C]), (T.SOB[15:128:16, 0:C], v("SOB", 0, C)[1]))
+        for k, (lo, hi) in enumerate(GCH):
+            if r < 2 and k == 1:
+                level_s(r + 1, 2)
             for b in range(4):
                 tt(v(XN, 4 * lo + b, 4 * hi, 4), ind(v("D", C * b, C * b + C), v(new, lo // 16, hi // 16)), v(X, 4 * lo + b, 4 * hi, 4), OP.add)
             quant_state(r + 1, k)

from concourse.bass import DstId, RemoteDMATransfer
from concourse.mybir import dt, AluOpType as OP, ActivationFunctionType as AF

C = 480
CH = [(0, 256), (256, 480)]
GCH = [(0, 320), (320, 480)]
MASK = [1, 2, 3]
TW = 1056

SCRATCH = {
    "UT": ("sbuf", [128, 512], "bfloat16"), "VT": ("sbuf", [128, 512], "bfloat16"),
    "X0": ("sbuf", [128, 4 * C], "bfloat16"), "X1": ("sbuf", [128, 4 * C], "bfloat16"),
    "X2": ("sbuf", [128, 4 * C], "bfloat16"), "X3": ("sbuf", [128, 4 * C], "bfloat16"),
    "XH": ("sbuf", [128, 4 * C], "bfloat16"), "G": ("sbuf", [128, 4 * C], "bfloat16"),
    "Z": ("sbuf", [128, 4 * C], "bfloat16"), "H": ("sbuf", [128, 4 * C], "bfloat16"),
    "D": ("sbuf", [128, 4 * C], "bfloat16"),
    "SE": ("sbuf", [128, 60], "int32"), "SN": ("sbuf", [128, 64], "float32"), "SPF": ("sbuf", [128, 32], "float32"),
    "DS": ("sbuf", [128, 32], "float32"),
    "TD": ("sbuf", [128, 224], "float32"), "TB": ("sbuf", [128, 224], "float32"),
    "FT": ("sbuf", [128, 224], "float32"), "FS": ("sbuf", [128, 224], "float32"), "FL": ("sbuf", [128, 224], "uint16"),
    "A": ("sbuf", [128, 544], "bfloat16"), "YB": ("sbuf", [128, 544], "bfloat16"), "YK": ("sbuf", [128, 544], "bfloat16"),
    "GA0": ("sbuf", [128, 544], "bfloat16"), "GA1": ("sbuf", [128, 544], "bfloat16"),
    "TT": ("sbuf", [128, 2 * TW], "bfloat16"), "T2": ("sbuf", [128, 2 * TW], "bfloat16"),
    "SM": ("sbuf", [128, 496], "bfloat16"),
    "CB": ("sbuf", [128, 2 * C], "bfloat16"), "EB": ("sbuf", [128, 2 * C], "bfloat16"), "EA": ("sbuf", [128, 2 * C], "bfloat16"),
    "Y2": ("sbuf", [128, C], "bfloat16"), "Y1": ("sbuf", [128, C], "bfloat16"), "Y4": ("sbuf", [128, C], "bfloat16"),
    "WK": ("sbuf", [128, C], "bfloat16"), "WL": ("sbuf", [128, C], "bfloat16"),
    "ID": ("sbuf", [128, C], "float32"), "ID1": ("sbuf", [128, C], "float32"), "IDB": ("sbuf", [128, C], "float32"),
    "LG": ("sbuf", [128, C], "float32"), "LV1": ("sbuf", [128, C], "float32"), "LV2": ("sbuf", [128, C], "float32"),
    "LV3": ("sbuf", [128, C], "float32"),
    "EN": ("sbuf", [128, C], "bfloat16"), "XX": ("sbuf", [128, C // 2], "bfloat16"), "DD": ("sbuf", [128, C // 2], "float32"),
    "XD": ("sbuf", [128, C // 2], "float32"), "RR": ("sbuf", [128, C], "float32"),
    "SOA": ("sbuf", [128, C], "float32"), "SOB": ("sbuf", [128, C], "float32"), "YO": ("sbuf", [128, C], "float32"),
    "K4": ("sbuf", [128, 64], "uint16"), "K6": ("sbuf", [128, 64], "uint16"),
    "IC": ("sbuf", [128, 8], "int32"), "CC": ("sbuf", [128, 48], "float32"), "SI": ("sbuf", [128, 32], "float32"),
    "SEL": ("sbuf", [128, 22], "uint16"), "UL": ("sbuf", [128, 8], "uint16"),
    "ONE": ("sbuf", [128, 128], "bfloat16"), "EYE": ("sbuf", [128, 128], "bfloat16"), "ET": ("sbuf", [128, 2048], "bfloat16"),
    "QU": ("sbuf", [128, 128], "float8_e4m3fn_x4"), "PU": ("sbuf", [128, 128], "uint8"),
    "QUP": ("sbuf", [128, 128], "float8_e4m3fn_x4"), "PUP": ("sbuf", [128, 128], "uint8"),
    "QV": ("sbuf", [128, 128], "float8_e4m3fn_x4"), "PV": ("sbuf", [128, 128], "uint8"),
    "QE": ("sbuf", [128, 512], "float8_e4m3fn_x4"), "PE": ("sbuf", [128, 512], "uint8"),
    "QW": ("sbuf", [128, 512], "float8_e4m3fn_x4"), "PW": ("sbuf", [128, 512], "uint8"),
    "QX": ("sbuf", [128, C], "float8_e4m3fn_x4"), "PX": ("sbuf", [128, C], "uint8"),
    "QO": ("sbuf", [128, C], "float8_e4m3fn_x4"), "PO": ("sbuf", [128, C], "uint8"),
    "QZ": ("sbuf", [128, C], "float8_e4m3fn_x4"), "PZ": ("sbuf", [128, C], "uint8"),
    "ps": ("psum", [128, 4096], "float32"),
}
for _r in range(4):
    SCRATCH["SU%d" % _r] = ("sbuf", [128, 64], "uint16")
for _r in range(3):
    SCRATCH["QH%d" % _r] = ("sbuf", [128, C], "float8_e4m3fn_x4")
    SCRATCH["PH%d" % _r] = ("sbuf", [128, C], "uint8")
    SCRATCH["LC%d" % _r] = ("sbuf", [128, C], "float8_e4m3fn_x4")
    SCRATCH["LS%d" % _r] = ("sbuf", [128, C], "uint8")
    SCRATCH["LL%d" % _r] = ("sbuf", [128, 64], "uint16")
NDMA = 32
SEMAPHORES = (["qv", "qs", "qt", "qg", "sent"] + ["dm%d" % k for k in range(NDMA)]
              + ["ar%d_%d" % (r, k) for r in range(3) for k in range(len(CH))] + ["ls%d" % r for r in range(3)])


def rank_program(g, core, T, topo):
    rank = T.rank_of(core)
    if rank is None:
        return
    eng = {"v": g.vector, "s": g.scalar, "t": g.tensor, "g": g, "y": g.sync}
    qsem = {"v": "qv", "s": "qs", "t": "qt", "g": "qg"}
    cnt = {"qv": 0, "qs": 0, "qt": 0, "qg": 0, "sent": 0}
    waited = {q: {} for q in eng}
    recs = {}
    ndma = [0]
    alldma = []

    def v(name, lo, hi, st=1):
        return T[name][:, lo:hi:st], [(name, lo, hi, st)]

    def ind(w, off):
        return w[0].indirect(off[0]), w[1] + off[1]

    def b8(w):
        return w[0].bitcast(dt.uint8), w[1]

    def b32(w):
        return w[0].bitcast(dt.uint32), w[1]

    def meets(a, b):
        if a[1] >= b[2] or b[1] >= a[2]:
            return False
        return not (a[3] == b[3] and a[3] > 1 and (a[1] - b[1]) % a[3])

    def wait(q, sem, val):
        if waited[q].get(sem, 0) < val:
            eng[q].wait_ge(T.sem[sem], val)
            waited[q][sem] = val

    def waits(q, outs, ins, anyway=False):
        need = {}
        for w, views in ((1, outs), (0, ins)):
            for view in views:
                for reg in view[1]:
                    hard = w or reg[0] == "ps"
                    if reg[0] == "ps":
                        reg = ("ps", reg[1] // 512 * 512, reg[1] // 512 * 512 + 512, 1)
                    for (rg, isw, sem, val, q2) in recs.get(reg[0], []):
                        if not meets(rg, reg) or not (isw or hard):
                            continue
                        if q2 == q and not anyway and not isw:
                            continue
                        need[sem] = max(need.get(sem, 0), val)
        for sem in need:
            wait(q, sem, need[sem])

    def note(outs, ins, sem, val, q2):
        for w, views in ((1, outs), (0, ins)):
            for view in views:
                for reg in view[1]:
                    if reg[0] == "ps":
                        reg = ("ps", reg[1] // 512 * 512, reg[1] // 512 * 512 + 512, 1)
                    l = recs.setdefault(reg[0], [])
                    if w or reg[0] == "ps":
                        l[:] = [x for x in l if not (x[0][1] >= reg[1] and x[0][2] <= reg[2] and (reg[3] == 1 or (x[0][3] == reg[3] and (x[0][1] - reg[1]) % reg[3] == 0)))]
                    l.append((reg, 1 if (w or reg[0] == "ps") else 0, sem, val, q2))

    def do(q, fn, outs, ins):
        waits(q, outs, ins)
        sem = qsem[q]
        cnt[sem] += 1
        fn(eng[q]).then_inc(T.sem[sem], 1)
        note(outs, ins, sem, cnt[sem], q)

    def dma(q, out, in_):
        waits(q, [out], [in_], True)
        sem = "dm%d" % ndma[0]
        ndma[0] += 1
        eng[q].dma_start(out[0], in_[0]).then_inc(T.sem[sem], 16)
        note([out], [in_], sem, 16, "dma" + sem)
        alldma.append(sem)

    def ext(ap):
        return ap, []

    def send(dst, out, in_, rsem):
        waits("g", [], [in_])
        rid, pid, _ = topo.addr(dst)
        m = topo.mask(core, dst)
        g.remote_dma(out[0], in_[0], T.sem[rsem], T.sem.sent, pid, rid, m)
        cnt["sent"] += len(topo.engines(core, dst))

    def lands(out, rsem, val):
        note([out], [], rsem, val, "remote")

    def tt(out, a, b, op):
        do("v", lambda e: e.tensor_tensor(out[0], a[0], b[0], op), [out], [a, b])

    def tsc(out, a, s1, s2, o0, o1=None):
        ins = [a] + [x for x in (s1, s2) if isinstance(x, tuple)]
        p = [x[0] if isinstance(x, tuple) else x for x in (s1, s2)]
        if o1 is None:
            do("v", lambda e: e.tensor_scalar(out[0], a[0], p[0], None, o0), [out], ins)
        else:
            do("v", lambda e: e.tensor_scalar(out[0], a[0], p[0], p[1], o0, o1), [out], ins)

    def tcp(out, a):
        do("v", lambda e: e.tensor_copy(out[0], a[0]), [out], [a])

    def act(out, a, func=AF.Copy, scale=1.0, bias=0.0):
        ins = [a] + [x for x in (scale, bias) if isinstance(x, tuple)]
        kw = {}
        if isinstance(scale, tuple) or scale != 1.0:
            kw["scale"] = scale[0] if isinstance(scale, tuple) else scale
        if isinstance(bias, tuple) or bias != 0.0:
            kw["bias"] = bias[0] if isinstance(bias, tuple) else bias
        do("s", lambda e: e.activation(out[0], a[0], func, **kw), [out], ins)

    def fill(out, c):
        do("v", lambda e: e.memset(out[0], c), [out], [])

    def quant(q, p, x):
        do("v", lambda e: e.quantize_mx(q[0], p[0], x[0]), [q, p], [x])

    bank = [0]

    def mm(lq, lp, rq, rp, n):
        o = v("ps", 512 * bank[0], 512 * bank[0] + n)
        bank[0] = (bank[0] + 1) % 8
        do("t", lambda e: e.matmul_mx(o[0], lq[0], lp[0], rq[0], rp[0], True, True), [o], [lq, lp, rq, rp])
        return o

    def turn(dst, at, src):
        do("v", lambda e: e.transpose(T[dst][:, at:at + C], T[src][:, 32:32 + C]), [v(dst, at, at + C)], [v(src, 32, 32 + C)])
        do("v", lambda e: e.transpose(T[dst][:, at + C:at + C + 512], T[src][:, 16:528]), [v(dst, at + C, at + C + 512)], [v(src, 16, 528)])

    def col(k):
        return v("CC", k, k + 1)

    def iota(out, pattern, base, cm):
        do("g", lambda e: e.iota(out[0], pattern, base, cm, allow_small_or_imprecise_dtypes=True), [out], [])

    dma("s", v("SE", 0, 60), ext(T.se[:]))
    for lo, hi in GCH:
        dma("y", v("X0", 4 * lo, 4 * hi), ext(T.x[:, 4 * lo:4 * hi]))
    dma("s", v("UT", 0, 512), ext(T.u[:]))
    dma("s", b8(v("QW", 0, 512)), ext(T.wc[:]))
    dma("s", v("PW", 0, 512), ext(T.ws[:]))
    dma("y", v("VT", 0, 512), ext(T.v[:]))

    do("g", lambda e: e.iota(T.IC[:, 0:1], [[0, 1]], 0, 1), [v("IC", 0, 1)], [])
    for at, n, row, step in ((0, 2, 7, 4), (4, 2, 5, 4), (8, 2, 14, -11), (12, 1, 3, 0), (14, 2, TW + 14, -TW - 13), (18, 2, 13, TW + 2)):
        iota(v("SI", at, at + 2 * n), [[step, n], [256, 2]], row, 0)
    iota(v("SI", 22, 30), [[16, 8]], 0, 0)
    iota(v("IDB", 0, C), [[1, C]], -240, 0)
    iota(v("ID", 0, C), [[1, C]], 0, 0)

    ic = lambda k: v("IC", k, k + 1)
    for k, sh, an in ((1, 0, 15), (2, 1, 1), (3, 2, 1), (4, 3, 1), (5, 4, 1), (6, 1, 7), (7, 0, 1)):
        tsc(ic(k), ic(0), sh, an, OP.logical_shift_right, OP.bitwise_and)
    tcp(v("CC", 0, 7), v("IC", 0, 7))
    tcp(col(35), ic(7))
    tsc(col(7), ic(7), -1.0, 1.0, OP.mult, OP.add)
    tsc(col(9), col(1), 1.0, None, OP.is_equal)
    tsc(col(30), col(1), 3.0, None, OP.is_equal)
    tsc(col(33), col(1), 15.0, None, OP.is_equal)
    tsc(col(15), col(4), -1.0, 1.0, OP.mult, OP.add)
    tsc(col(11), col(2), -1.0, 1.0, OP.mult, OP.add)
    tsc(col(31), col(6), col(30), col(33), OP.subtract, OP.subtract)
    tsc(col(16), col(9), 2.0, None, OP.mult)
    tsc(col(10), col(2), col(7), None, OP.mult)
    tsc(col(8), col(15), col(7), None, OP.mult)
    tsc(col(34), col(31), col(35), col(7), OP.mult, OP.add)
    tsc(col(17), col(15), col(7), col(16), OP.mult, OP.add)
    tsc(col(12), col(11), col(7), None, OP.mult)
    tsc(v("UL", 0, 8), v("SI", 22, 30), col(34), None, OP.add)

    fill(v("SN", 0, 64), 0.0)
    fill(v("SM", 0, 496), 1.0)
    fill(v("SM", 0, 496, 8), 0.0)
    tcp(v("SN", 0, 30), v("SE", 0, 30))
    tcp(v("SN", 32, 62), v("SE", 30, 60))
    tcp(v("SU0", 0, 64), v("SN", 0, 64))

    def send_lists(r):
        dst = T.cores[rank ^ MASK[r]]
        send(dst, v("LL%d" % r, 0, 64), v("SU%d" % r, 0, 64), "ls%d" % r)
        lands(v("LL%d" % r, 0, 64), "ls%d" % r, len(topo.engines(dst, core)))

    send_lists(0)
    for b, lo, hi in [("A", 0, 32), ("A", 512, 544), ("TT", 992, TW), ("YB", 0, 32), ("YB", 512, 544), ("TT", TW, 2 * TW), ("YK", 0, 32),
                      ("YK", 512, 544), ("GA0", 0, 32), ("GA0", 512, 544), ("GA1", 0, 32), ("GA1", 512, 544), ("T2", 992, TW),
                      ("T2", TW + 992, 2 * TW), ("ET", 0, 2048)]:
        iota(v(b, lo, hi), [[0, hi - lo]], 0, 0)
    iota(v("ONE", 0, 128), [[0, 128]], 1, 0)
    do("g", lambda e: e.affine_select(T.EYE[:, 0:128], T.ONE[:, 0:128], [[-1, 128]], OP.is_equal, 0.0, 0, 1), [v("EYE", 0, 128)], [v("ONE", 0, 128)])

    def tables():
        tt(v("DS", 0, 32), v("SN", 32, 64), v("SN", 0, 32), OP.subtract)
        act(v("TB", 0, 32), v("SN", 0, 32))
        act(v("TB", 32, 64), v("SN", 0, 32))
        act(v("TD", 128, 160), v("DS", 0, 32))
        act(v("TD", 160, 192), v("DS", 0, 32))
        act(v("TB", 64, 128), v("TB", 0, 64))
        act(v("TB", 128, 192), v("TB", 0, 64))
        act(v("TD", 0, 64), v("TD", 128, 192), bias=480.0)
        act(v("TD", 64, 128), v("TD", 128, 192), bias=480.0)

    tables()
    quant(v("QU", 0, 128), v("PU", 0, 128), v("UT", 0, 512))
    tcp(b32(v("QUP", 0, 128)), ind(b32(v("QU", 0, 128)), v("UL", 0, 8)))
    tcp(v("PUP", 0, 128), ind(v("PU", 0, 128), v("UL", 0, 8)))

    def quant_state(r, k):
        lo, hi = GCH[k]
        q, p = ("QX", "PX") if r < 3 else ("QO", "PO")
        quant(v(q, lo, hi), v(p, lo, hi), v("X%d" % r, 4 * lo, 4 * hi))

    def signs(k):
        lo, hi = GCH[k]
        s = mm(v("QUP", 0, 128), v("PUP", 0, 128), v("QX", lo, hi), v("PX", lo, hi), hi - lo)
        tsc(v("A", 32 + lo, 32 + hi), s, 0.0, col(17), OP.is_gt, OP.not_equal)

    def half_state(r, k):
        lo, hi = GCH[k]
        for b in range(4):
            act(v("XH", C * b + lo, C * b + hi), v("X%d" % r, 4 * lo + b, 4 * hi, 4), scale=0.5)

    for k in range(len(GCH)):
        quant_state(0, k)

    tsc(col(25), col(35), col(5), None, OP.not_equal)
    tsc(col(26), col(5), -32.0, 512.0, OP.mult, OP.add)
    tsc(col(14), col(3), -1.0, 1.0, OP.mult, OP.add)
    tsc(col(27), col(25), col(26), None, OP.mult)
    signs(0)
    tsc(col(13), col(3), col(7), col(9), OP.mult, OP.add)
    tsc(col(14), col(14), col(7), col(9), OP.mult, OP.add)
    tsc(col(28), col(5), 16.0, col(27), OP.mult, OP.add)
    signs(1)
    act(v("CB", 0, C), v("IDB", 0, C), AF.Identity, scale=col(9), bias=col(12))
    act(v("CB", C, 2 * C), v("IDB", 0, C), AF.Identity, scale=col(9), bias=col(10))
    act(v("ID1", 0, C), v("ID", 0, C), scale=col(11))
    turn("TT", 0, "A")
    tsc(col(29), col(6), 32.0, col(28), OP.mult, OP.add)
    tsc(v("SEL", 0, 22), v("SI", 0, 22), col(29), None, OP.add)

    def more_constants():
        tsc(col(18), col(3), -512.0, -240.0, OP.mult, OP.add)
        tsc(col(22), col(3), 2512.0, -2000.0, OP.mult, OP.add)
        tsc(col(23), col(4), 3024.0, -2000.0, OP.mult, OP.add)
        tsc(col(19), col(4), -1024.0, col(18), OP.mult, OP.add)
        tsc(col(21), col(18), col(8), col(9), OP.mult, OP.add)
        tsc(col(20), col(19), col(7), col(9), OP.mult, OP.add)

    def tables_partner(r):
        L = "LL%d" % r
        tcp(v("SPF", 0, 32), v(L, 0, 32))
        tcp(v("TB", 192, 224), v(L, 32, 64))
        tt(v("TD", 192, 224), v("SPF", 0, 32), v("TB", 192, 224), OP.subtract)

    def offsets(a, b):
        lo, hi = 32 * a, 32 * b
        tt(v("FT", lo, hi), ind(v("TT", 0, TW), v("SEL", 2 * a, 2 * b)), v("TD", lo, hi), OP.mult)
        tt(v("FS", lo, hi), v("FT", lo, hi), v("TB", lo, hi), OP.add)
        tcp(v("FL", lo, hi), v("FS", lo, hi))

    def fl(k):
        return v("FL", 32 * k, 32 * k + 30)

    def level_s(r, k):
        s0 = v("LL%d" % r, 0, 30)
        if k == 1:
            act(v("LG", 0, C), ind(v("ID", 0, C), s0), scale=col(2))
        else:
            act(v("LG", 0, C), ind(v("LV%d" % (k - 1), 0, C), s0), AF.Identity, bias=col(20 + k))

    def level_v(r, k):
        s1 = v("LL%d" % r, 32, 62)
        if k == 1:
            tt(v("LV1", 0, C), ind(v("ID1", 0, C), s1), v("LG", 0, C), OP.add)
        else:
            tt(v("LV%d" % k, 0, C), ind(v("LV%d" % (k - 1), 0, C), s1), v("LG", 0, C), OP.max)

    def numbers(src, dst):
        turn("TT", 0, src)
        o, d, m = v("TT", TW, TW + 992, 2), v("TT", 0, 992, 2), v("SM", 0, 496)
        do("v", lambda e: e.tensor_tensor_scan(o[0], m[0], d[0], 0.0, OP.mult, OP.add), [o], [m, d])
        tsc(v(dst, 0, 64), ind(v("TT", 0, 2 * TW), v("SEL", 14, 18)), 240.0, None, OP.add)

    def outputs(k):
        lo, hi = GCH[k]
        o = mm(v("QV", 0, 128), v("PV", 0, 128), v("QO", lo, hi), v("PO", lo, hi), hi - lo)
        dma("y", ext(T.oc[:, 4 * lo:4 * hi]), b8(v("QO", lo, hi)))
        act(v("YO", lo, hi), o)
        for j in range(4):
            dma("s" if j % 2 else "y", ext(T.osc[4 * j:4 * j + 4, lo:hi]), (T.PO[32 * j:32 * j + 4, lo:hi], v("PO", lo, hi)[1]))
        dma("s", ext(T.y[:, lo:hi]), v("YO", lo, hi))

    for r in range(3):
        partner = T.cores[rank ^ MASK[r]]
        X, XN = "X%d" % r, "X%d" % (r + 1)
        if r == 0:
            level_s(0, 1)
        else:
            turn("TT", 0, "A")
        offsets(0, 2)
        act(v("EB", 0, C), ind(v("CB", 0, 2 * C), fl(0)), scale=col(14))
        act(v("EB", C, 2 * C), ind(v("CB", 0, 2 * C), fl(0)), scale=col(13))
        if r == 0:
            offsets(2, 6)
            level_v(0, 1)
            tables_partner(0)
            offsets(6, 7)
            more_constants()
            level_s(0, 2)
            level_v(0, 2)
            level_s(0, 3)
        else:
            offsets(2, 7)
            level_v(r, 3)
        act(v("EA", 0, C), ind(v("CB", 0, 2 * C), fl(1)), scale=col(14))
        tcp(v("Y2", 0, C), ind(v("EB", 0, 2 * C), fl(2)))
        if r == 0:
            level_v(0, 3)
        tt(v("Y1", 0, C), ind(v("Y2", 0, C), fl(4)), v("A", 32, 32 + C), OP.mult)
        act(v("WK", 0, C), ind(v("LV3", 0, C), fl(6)), AF.Identity, scale=col(7), bias=col(20))
        act(v("EA", C, 2 * C), ind(v("CB", 0, 2 * C), fl(1)), scale=col(13))
        act(v("Y4", 0, C), ind(v("EA", 0, 2 * C), fl(3)))
        tt(v("YB", 32, 32 + C), ind(v("Y1", 0, C), fl(5)), v("WK", 0, C), OP.mult)
        if r == 0:
            for b in range(4):
                act(v("ET", 512 * b + b, 512 * b + 512, 4), v("EYE", 0, 128))
        if r == 2:
            quant(v("QV", 0, 128), v("PV", 0, 128), v("VT", 0, 512))
        numbers("YB", "K4")
        for lo, hi in CH:
            act(v("WL", lo, hi), ind(v("LV2", 0, C), v("K4", lo // 16, hi // 16)), AF.Identity, scale=col(8), bias=col(21))
        tt(v("DD", 0, 240), v("LV1", 1, C, 2), v("LV1", 0, C, 2), OP.subtract)
        for lo, hi in CH:
            tt(v("YK", 32 + lo, 32 + hi), ind(v("Y4", 0, C), v("K4", 32 + lo // 16, 32 + hi // 16)), v("WL", lo, hi), OP.mult)
        if r == 0:
            for k in range(len(GCH)):
                half_state(0, k)
        numbers("YK", "K6")
        if r == 0:
            quant(v("QE", 0, 512), v("PE", 0, 512), v("ET", 0, 2048))
        for lo, hi in CH:
            for b in range(4):
                act(v("G", C * b + lo, C * b + hi), ind(v("XH", C * b, C * b + C), v("K6", 32 + lo // 16, 32 + hi // 16)))
        for lo, hi in CH:
            for b in range(4):
                tt(v("Z", 4 * lo + b, 4 * hi, 4), ind(v("XH", C * b, C * b + C), v("K6", lo // 16, hi // 16)), v("G", C * b + lo, C * b + hi), OP.add)
            quant(v("QZ", lo, hi), v("PZ", lo, hi), v("Z", 4 * lo, 4 * hi))
        for k, (lo, hi) in enumerate(CH):
            for b in range(4):
                s = mm(v("QW", 128 * b, 128 * b + 128), v("PW", 128 * b, 128 * b + 128), v("QZ", lo, hi), v("PZ", lo, hi), hi - lo)
                h = v("H", 4 * lo + b, 4 * hi, 4)
                if k == 0 or b == 0:
                    act(h, s, scale=0.03125)
                else:
                    tsc(h, s, 0.03125, None, OP.mult)
            quant(v("QH%d" % r, lo, hi), v("PH%d" % r, lo, hi), v("H", 4 * lo, 4 * hi))
            sem = "ar%d_%d" % (r, k)
            send(partner, b8(v("LC%d" % r, lo, hi)), b8(v("QH%d" % r, lo, hi)), sem)
            send(partner, v("LS%d" % r, lo, hi), v("PH%d" % r, lo, hi), sem)
            n = 2 * len(topo.engines(partner, core))
            lands(v("LC%d" % r, lo, hi), sem, n)
            lands(v("LS%d" % r, lo, hi), sem, n)
        act(v("EN", 0, C), ind(v("A", 32, 32 + C), v("K6", 0, 30)))
        tt(v("XX", 0, 240), v("EN", 0, C, 2), v("EN", 1, C, 2), OP.not_equal)
        tt(v("XD", 0, 240), v("XX", 0, 240), v("DD", 0, 240), OP.mult)
        tt(v("RR", 0, C, 2), v("LV1", 0, C, 2), v("XD", 0, 240), OP.add)
        tt(v("RR", 1, C, 2), v("LV1", 1, C, 2), v("XD", 0, 240), OP.subtract)
        own0, own1 = v("SU%d" % r, 0, 30), v("SU%d" % r, 32, 62)
        act(v("GA0", 32, 32 + C), ind(v("RR", 0, C), own0), bias=-240.0)
        if r < 2:
            tsc(v("GA1", 32, 32 + C), ind(v("RR", 0, C), own1), -240.0, None, OP.add)
        turn("T2", 0, "GA0")
        if r < 2:
            turn("T2", TW, "GA1")
        tsc(v("SN", 0, 64), ind(v("T2", 0, 2 * TW), v("SEL", 18, 22)), 240.0, None, OP.add)
        new = "SU%d" % (r + 1)
        tcp(v(new, 0, 64), v("SN", 0, 64))
        if r < 2:
            send_lists(r + 1)
        for k, (lo, hi) in enumerate(CH):
            for b in range(4):
                s = mm(v("QE", 128 * b, 128 * b + 128), v("PE", 128 * b, 128 * b + 128), v("LC%d" % r, lo, hi), v("LS%d" % r, lo, hi), hi - lo)
                act(v("D", C * b + lo, C * b + hi), s)
        if r < 2:
            level_s(r + 1, 1)
            tables()
        else:
            act(v("SOA", 0, C), ind(v("RR", 0, C), own0))
            act(v("SOB", 0, C), ind(v("RR", 0, C), own1))
            dma("y", ext(T.so[:, 0:C]), (T.SOA[13:128:16, 0:C], v("SOA", 0, C)[1]))
            dma("y", ext(T.so[:, C:2 * C]), (T.SOB[15:128:16, 0:C], v("SOB", 0, C)[1]))
        for k, (lo, hi) in enumerate(GCH):
            if r < 2 and k == 1:
                level_s(r + 1, 2)
            for b in range(4):
                tt(v(XN, 4 * lo + b, 4 * hi, 4), ind(v("D", C * b, C * b + C), v(new, lo // 16, hi // 16)), v(X, 4 * lo + b, 4 * hi, 4), OP.add)
            quant_state(r + 1, k)
            if r < 2:
                half_state(r + 1, k)
                if k == 0:
                    level_v(r + 1, 1)
                else:
                    signs(0)
                    level_v(r + 1, 2)
                    level_s(r + 1, 3)
                    tables_partner(r + 1)
                    signs(1)
            else:
                outputs(k)

    for sem in alldma:
        wait("g", sem, 16)
    for sem in cnt:
        if cnt[sem]:
            wait("g", sem, cnt[sem])
